import numpy as np
import ml_dtypes


def mxq(x, axis, fmt="e4m3"):
    dtype, down = {"e4m3": (ml_dtypes.float8_e4m3fn, 7), "e5m2": (ml_dtypes.float8_e5m2, 14)}[fmt]
    v = np.moveaxis(np.asarray(x, np.float32).astype(ml_dtypes.bfloat16).astype(np.float64), axis, -1)
    blocks = v.reshape(v.shape[:-1] + (-1, 32))
    amax = np.abs(blocks).max(-1, keepdims=True)
    byte = np.maximum(np.where(amax > 0, np.frexp(amax)[1] - 1 + 127, 0) - down, 1)
    scale = np.exp2(byte - 127.0)
    codes = (blocks / scale).astype(np.float32).astype(dtype).astype(np.float64)
    return np.moveaxis((codes * scale).reshape(v.shape), -1, axis)


WIDE = False


def mx_kscale(k):
    if not WIDE:
        return np.ones(k)
    levels = np.array([10, -10, 5, -5, 0])
    if k % 512:
        return np.exp2(np.random.permutation(np.resize(levels, k // 32))).repeat(32)
    a = np.empty((k // 512, 16))
    for p in range(k // 512):
        a[p, :8] = np.random.permutation(np.resize(levels, 8))
        for g in range(8):
            far = levels[np.abs(levels - a[p, g]) >= 10]
            a[p, g + 8] = far[np.random.randint(len(far))]
    return np.exp2(a.ravel()).repeat(32)


def f64(x):
    return np.asarray(x).astype(np.float64)


def striped(idx):
    return np.tile(np.asarray(idx).reshape(-1, 16).T, (8, 1)).astype(np.uint16)


def unstriped(offs):
    return offs[:16].T.reshape(-1).astype(np.int64)


D, T, I, M = 512, 2048, 512, 512


def setup_inputs():
    n = np.random.standard_normal
    idx = np.random.permutation(T)[:I]
    fd = mx_kscale(D)
    fi = mx_kscale(I)
    return {
        "keys": (n((D, T)) / fd[:, None]).astype(np.float32),
        "cent": (n((D, M)) * 0.7 / np.sqrt(D) * fd[:, None]).astype(np.float32),
        "fac": (np.random.uniform(8.0, 32.0, (I, 1)) * fi[:, None]).astype(np.float32),
        "ksc": (np.random.uniform(0.5, 2.0, (I, 1)) / fi[:, None]).astype(np.float32),
        "dsc": (np.random.uniform(0.5, 2.0, (1, D)) * fd).astype(np.float32),
        "offs": striped(idx),
    }


def reference(keys, cent, fac, ksc, dsc, offs):
    idx = unstriped(offs)
    keysidxq = mxq(f64(keys)[:, idx], 0, "e4m3")
    centq = mxq(f64(cent), 0, "e4m3")
    a = keysidxq.T @ centq
    p = np.exp(a - np.max(a, axis=1, keepdims=True))
    w = p * f64(fac) / np.sum(p, axis=1, keepdims=True)
    kt = f64(keys)[:, idx].T
    ks = kt * f64(ksc) * f64(dsc)
    ksq = mxq(ks, 0, "e4m3")
    wq = mxq(w, 0, "e4m3")
    y = ksq.T @ wq
    return y

@@ -1,0 +1,214 @@
+from contextlib import ExitStack
+
+import concourse.mybir as mybir
+from concourse.masks import make_identity
+
+D, T, I, M = 512, 2048, 512, 512
+FLOPS = 2 * D * I * M * 2
+
+F32 = mybir.dt.float32
+BF16 = mybir.dt.bfloat16
+U32 = mybir.dt.uint32
+U16 = mybir.dt.uint16
+U8 = mybir.dt.uint8
+FP8X4 = mybir.dt.float8_e4m3fn_x4
+ACT = mybir.ActivationFunctionType
+ALU = mybir.AluOpType
+AXIS = mybir.AxisListType
+
+P = 128
+PACK = 4
+HALF = M // 2
+
+
+def tile_attend_softcluster_kernel(tc, keys, cent, fac, ksc, dsc, offs, out):
+    nc = tc.nc
+    with ExitStack() as ctx:
+        sb = ctx.enter_context(tc.tile_pool(name="sb", bufs=1))
+        ps = ctx.enter_context(tc.psum_pool(name="ps", bufs=1))
+
+        offsets = sb.tile([P, I // 16], U16, name="offsets")
+        nc.sync.dma_start(offsets[:], offs)
+
+        key_rows = keys.rearrange("(p t) n -> p t n", t=PACK)
+        pool_t = [sb.tile([P, T], F32, name="pool%d" % t) for t in range(PACK)]
+        nc.sync.dma_start(out=pool_t[0][:], in_=key_rows[:, 0, :])
+        ksc4 = sb.tile([P, PACK], F32, name="ksc4")
+        dsc4 = sb.tile([P, PACK], F32, name="dsc4")
+        fac4 = sb.tile([P, PACK], F32, name="fac4")
+        nc.scalar.dma_start(out=ksc4[:], in_=ksc.rearrange("(s r) o -> s (r o)", r=PACK))
+        nc.scalar.dma_start(out=dsc4[:], in_=dsc.rearrange("o (p t) -> p (o t)", t=PACK))
+        for t in range(1, PACK):
+            nc.sync.dma_start(out=pool_t[t][:], in_=key_rows[:, t, :])
+        cent_rows = cent.rearrange("(p t) m -> p t m", t=PACK)
+        cent_raw = [sb.tile([P, PACK, HALF], F32, name="cent_raw%d" % h) for h in range(2)]
+        for h in range(2):
+            nc.sync.dma_start(out=cent_raw[h][:], in_=cent_rows[:, :, h * HALF : (h + 1) * HALF])
+        nc.sync.dma_start(out=fac4[:], in_=fac.rearrange("(s r) o -> s (r o)", r=PACK))
+
+        warm_in = sb.tile([P, 1], F32, name="warm_in")
+        warm_out = sb.tile([P, 1], F32, name="warm_out")
+        nc.vector.memset(warm_in[:], 0.0)
+        nc.scalar.activation(warm_out[:], warm_in[:], ACT.Exp)
+
+        ident = sb.tile([P, P], F32, name="ident")
+        make_identity(nc, ident[:])
+
+        ksc_bank = ps.tile([P, PACK, P], F32, name="ksc_bank", tag="bank4")
+        for r in range(PACK):
+            nc.tensor.transpose(ksc_bank[:, r, :], ksc4[:, r : r + 1].to_broadcast([P, P]), ident[:])
+        picked = [sb.tile([P, 2, I], F32, name="picked%d" % u) for u in range(2)]
+        last_both = sb.tile([P, I], F32, name="last_both")
+        both = [picked[(t + 1) // 2][:, (t + 1) % 2, :] for t in range(PACK - 1)] + [last_both[:]]
+        for t in range(PACK):
+            nc.scalar.activation(
+                both[t].rearrange("p (s r) -> p s r", r=PACK),
+                ksc_bank[:].rearrange("p r s -> p s r"),
+                ACT.Copy,
+                scale=dsc4[:, t : t + 1],
+            )
+
+        key_bf = sb.tile([P, PACK, P, PACK], BF16, name="key_bf", align_bytes=64)
+        key_codes = sb.tile([P, I], U32, name="key_codes", align_bytes=64)
+        key_scales = sb.tile([P, I], U8, name="key_scales", align_bytes=64)
+        ks_in = [sb.tile([P, 2 * I], BF16, name="ks_in%d" % u, align_bytes=64) for u in range(2)]
+        ks_codes = [sb.tile([P, 2 * P], U32, name="ks_codes%d" % u, align_bytes=64) for u in range(2)]
+        ks_scales = []
+
+        def gather(t):
+            nc.vector.tensor_copy(picked[t // 2][:, t % 2, :], pool_t[t][:].indirect(offsets[:]))
+
+        def weave_keys(copy, u):
+            copy(
+                key_bf[:, :, :, 2 * u : 2 * u + 2].rearrange("p r s e -> p s e r"),
+                picked[u][:].rearrange("p e (s r) -> p s e r", r=PACK),
+            )
+
+        def scaled_keys(t):
+            ks_bf = sb.tile([P, I], BF16, name="ks_bf%d" % t, tag="stage%d" % min(t, 2), align_bytes=64)
+            nc.vector.tensor_tensor(ks_bf[:], picked[t // 2][:, t % 2, :], both[t], ALU.mult)
+            words = ks_bf[:].bitcast(F32)
+            turned = ps.tile([P, 2, P], F32, name="turned%d" % t, tag="bank%d" % (5 + t if t < 3 else 2))
+            for u in range(2):
+                nc.tensor.transpose(turned[:, u, :], words[:, u : I // 2 : 2], ident[:])
+            nc.scalar.copy(
+                ks_in[t // 2][:, (t % 2) * I : (t % 2 + 1) * I].bitcast(F32).rearrange("s (p u) -> s p u", u=2),
+                turned[:].rearrange("s u p -> s p u"),
+            )
+
+        def quantize_scaled_keys(u):
+            ks_scales.append(sb.tile([P, 2 * P], U8, name="ks_scales%d" % u, tag="late%d" % (3 * u), align_bytes=64))
+            nc.vector.quantize_mx(out=ks_codes[u][:].bitcast(FP8X4), scales=ks_scales[u][:], in_=ks_in[u][:])
+
+        for t in range(PACK - 1):
+            gather(t)
+            scaled_keys(t)
+            if t == 1:
+                quantize_scaled_keys(0)
+                weave_keys(nc.scalar.copy, 0)
+        gather(PACK - 1)
+        weave_keys(nc.vector.tensor_copy, 1)
+        nc.vector.quantize_mx(
+            out=key_codes[:].bitcast(FP8X4),
+            scales=key_scales[:],
+            in_=key_bf[:].rearrange("p r s t -> p (r s t)"),
+        )
+
+        cent_codes = sb.tile([P, M], U32, name="cent_codes", align_bytes=64)
+        cent_scales = sb.tile([P, M], U8, name="cent_scales", align_bytes=64)
+        cent_all = sb.tile([P, M * PACK], BF16, name="cent_all", tag="stage2", align_bytes=64)
+        for h in range(2):
+            cent_bf = cent_all[:, h * HALF * PACK : (h + 1) * HALF * PACK]
+            nc.scalar.copy(
+                cent_bf.rearrange("p (c j t) -> p c t j", j=4, t=PACK),
+                cent_raw[h][:].rearrange("p t (c j) -> p c t j", j=4),
+            )
+            cols = slice(h * HALF, (h + 1) * HALF)
+            nc.vector.quantize_mx(out=cent_codes[:, cols].bitcast(FP8X4), scales=cent_scales[:, cols], in_=cent_bf)
+
+        neg_max = sb.tile([P, PACK], F32, name="neg_max")
+        sums = sb.tile([P, PACK], F32, name="sums")
+        inv = sb.tile([P, PACK], F32, name="inv")
+        shares = [sb.tile([P, M], F32, name="shares%d" % r, tag="late%d" % (r if r else 4), align_bytes=64) for r in range(PACK)]
+        scores = [ps.tile([P, M], F32, name="scores%d" % r, tag="bank%d" % r) for r in range(PACK)]
+        w_pair = sb.tile([P, 2, M, 2], BF16, name="w_pair")
+
+        def score(r):
+            cols = slice(r * P, (r + 1) * P)
+            nc.tensor.matmul_mx(
+                out=scores[r][:],
+                lhsT=key_codes[:, cols].bitcast(FP8X4),
+                lhsT_scale=key_scales[:, cols],
+                rhs=cent_codes[:].bitcast(FP8X4),
+                rhs_scale=cent_scales[:],
+                start=True,
+                stop=True,
+            )
+            nc.vector.tensor_reduce(neg_max[:, r : r + 1], scores[r][:], AXIS.X, ALU.max, negate=True)
+            nc.scalar.activation(
+                shares[r][:], scores[r][:], ACT.Exp, bias=neg_max[:, r : r + 1], accum_out=sums[:, r : r + 1]
+            )
+
+        def invert(r0, r1):
+            nc.vector.reciprocal(inv[:, r0:r1], sums[:, r0:r1])
+
+        def weigh(r, cols):
+            nc.vector.tensor_scalar(
+                w_pair[:, r // 2, cols, r % 2],
+                shares[r][:, cols],
+                inv[:, r : r + 1],
+                fac4[:, r : r + 1],
+                ALU.mult,
+                ALU.mult,
+            )
+
+        every = slice(0, M)
+        for r in range(3):
+            score(r)
+        invert(0, 1)
+        score(3)
+        invert(1, 3)
+        weigh(0, every)
+        weigh(1, every)
+        invert(3, 4)
+        scaled_keys(PACK - 1)
+        weigh(2, every)
+        for h in range(2):
+            weigh(3, slice(h * HALF, (h + 1) * HALF))
+
+        w_in = [sb.tile([P, HALF * PACK], BF16, name="w_in%d" % h, align_bytes=64) for h in range(2)]
+        w_codes = [sb.tile([P, HALF], U32, name="w_codes%d" % h, align_bytes=64) for h in range(2)]
+        w_scales = [sb.tile([P, HALF], U8, name="w_scales%d" % h, align_bytes=64) for h in range(2)]
+        nc.vector.tensor_copy(
+            w_in[0][:].rearrange("s (m u e) -> s m u e", u=2, e=2),
+            w_pair[:, :, 0:HALF, :].rearrange("s u m e -> s m u e"),
+        )
+        quantize_scaled_keys(1)
+        nc.scalar.copy(
+            w_in[1][:].rearrange("s (m u e) -> s m u e", u=2, e=2),
+            w_pair[:, :, HALF:M, :].rearrange("s u m e -> s m u e"),
+        )
+        for h in range(2):
+            nc.vector.quantize_mx(out=w_codes[h][:].bitcast(FP8X4), scales=w_scales[h][:], in_=w_in[h][:])
+
+
+        out_rows = out.rearrange("(p t) m -> p t m", t=PACK)
+        for h in range(2):
+            for u in range(2):
+                acc = ps.tile([P, 2, HALF], F32, name="acc%d%d" % (h, u), tag="bank%d" % (2 * h + u))
+                for e in range(2):
+                    nc.tensor.matmul_mx(
+                        out=acc[:, e, :],
+                        lhsT=ks_codes[u][:, e * P : (e + 1) * P].bitcast(FP8X4),
+                        lhsT_scale=ks_scales[u][:, e * P : (e + 1) * P],
+                        rhs=w_codes[h][:].bitcast(FP8X4),
+                        rhs_scale=w_scales[h][:],
+                        start=True,
+                        stop=True,
+                    )
+                res = sb.tile([P, 2, HALF], F32, name="res%d%d" % (h, u))
+                if u == 1:
+                    nc.vector.tensor_copy(res[:], acc[:])
+                else:
+                    nc.scalar.copy(res[:], acc[:])
+                nc.sync.dma_start(out=out_rows[:, 2 * u : 2 * u + 2, h * HALF : (h + 1) * HALF], in_=res[:])

@@ -28,11 +28,11 @@ def tile_attend_softcluster_kernel(tc, keys, cent, fac, ksc, dsc, offs, out):
         ps = ctx.enter_context(tc.psum_pool(name="ps", bufs=1))
 
         offsets = sb.tile([P, I // 16], U16, name="offsets")
-        nc.sync.dma_start(offsets[:], offs)
 
         key_rows = keys.rearrange("(p t) n -> p t n", t=PACK)
         pool_t = [sb.tile([P, T], F32, name="pool%d" % t) for t in range(PACK)]
         nc.sync.dma_start(out=pool_t[0][:], in_=key_rows[:, 0, :])
+        nc.sync.dma_start(offsets[:], offs)
         ksc4 = sb.tile([P, PACK], F32, name="ksc4")
         dsc4 = sb.tile([P, PACK], F32, name="dsc4")
         fac4 = sb.tile([P, PACK], F32, name="fac4")
@@ -41,9 +41,9 @@ def tile_attend_softcluster_kernel(tc, keys, cent, fac, ksc, dsc, offs, out):
         for t in range(1, PACK):
             nc.sync.dma_start(out=pool_t[t][:], in_=key_rows[:, t, :])
         cent_rows = cent.rearrange("(p t) m -> p t m", t=PACK)
-        cent_raw = [sb.tile([P, PACK, HALF], F32, name="cent_raw%d" % h) for h in range(2)]
-        for h in range(2):
-            nc.sync.dma_start(out=cent_raw[h][:], in_=cent_rows[:, :, h * HALF : (h + 1) * HALF])
+        cent_raw = [sb.tile([P, PACK, P], F32, name="cent_raw%d" % h, tag="raw%d" % h, align_bytes=64) for h in range(4)]
+        for h in range(4):
+            nc.sync.dma_start(out=cent_raw[h][:], in_=cent_rows[:, :, h * P : (h + 1) * P])
         nc.sync.dma_start(out=fac4[:], in_=fac.rearrange("(s r) o -> s (r o)", r=PACK))
 
         warm_in = sb.tile([P, 1], F32, name="warm_in")
@@ -58,9 +58,17 @@ def tile_attend_softcluster_kernel(tc, keys, cent, fac, ksc, dsc, offs, out):
         for r in range(PACK):
             nc.tensor.transpose(ksc_bank[:, r, :], ksc4[:, r : r + 1].to_broadcast([P, P]), ident[:])
         picked = [sb.tile([P, 2, I], F32, name="picked%d" % u) for u in range(2)]
-        last_both = sb.tile([P, I], F32, name="last_both")
-        both = [picked[(t + 1) // 2][:, (t + 1) % 2, :] for t in range(PACK - 1)] + [last_both[:]]
-        for t in range(PACK):
+        both = [picked[(t + 1) // 2][:, (t + 1) % 2, :] for t in range(PACK - 1)]
+        dsc_bank = ps.tile([P, P], F32, name="dsc_bank", tag="bank7")
+        nc.tensor.transpose(dsc_bank[:], dsc4[:, PACK - 1 : PACK].to_broadcast([P, P]), ident[:])
+        last_both = sb.tile([P, P, PACK], F32, name="last_both")
+        nc.vector.tensor_tensor(
+            last_both[:],
+            dsc_bank[:].unsqueeze(2).to_broadcast([P, P, PACK]),
+            ksc4[:].unsqueeze(1).to_broadcast([P, P, PACK]),
+            ALU.mult,
+        )
+        for t in range(PACK - 1):
             nc.scalar.activation(
                 both[t].rearrange("p (s r) -> p s r", r=PACK),
                 ksc_bank[:].rearrange("p r s -> p s r"),
@@ -69,10 +77,9 @@ def tile_attend_softcluster_kernel(tc, keys, cent, fac, ksc, dsc, offs, out):
             )
 
         key_bf = sb.tile([P, PACK, P, PACK], BF16, name="key_bf", align_bytes=64)
-        key_codes = sb.tile([P, I], U32, name="key_codes", align_bytes=64)
-        key_scales = sb.tile([P, I], U8, name="key_scales", align_bytes=64)
-        ks_in = [sb.tile([P, 2 * I], BF16, name="ks_in%d" % u, align_bytes=64) for u in range(2)]
-        ks_codes = [sb.tile([P, 2 * P], U32, name="ks_codes%d" % u, align_bytes=64) for u in range(2)]
+        key_codes = [sb.tile([P, HALF], U32, name="key_codes%d" % u, align_bytes=64) for u in range(2)]
+        key_scales = []
+        ks_codes = [sb.tile([P, P], U32, name="ks_codes%d" % t, align_bytes=64) for t in range(PACK)]
         ks_scales = []
 
         def gather(t):
@@ -85,60 +92,94 @@ def tile_attend_softcluster_kernel(tc, keys, cent, fac, ksc, dsc, offs, out):
             )
 
         def scaled_keys(t):
-            ks_bf = sb.tile([P, I], BF16, name="ks_bf%d" % t, tag="stage%d" % min(t, 2), align_bytes=64)
+            ks_bf = sb.tile([P, I], BF16, name="ks_bf%d" % t, tag="stage%d" % t, align_bytes=64)
             nc.vector.tensor_tensor(ks_bf[:], picked[t // 2][:, t % 2, :], both[t], ALU.mult)
             words = ks_bf[:].bitcast(F32)
-            turned = ps.tile([P, 2, P], F32, name="turned%d" % t, tag="bank%d" % (5 + t if t < 3 else 2))
+            turned = ps.tile([P, 2, P], F32, name="turned%d" % t, tag="bank%d" % (5 + t % 2))
             for u in range(2):
                 nc.tensor.transpose(turned[:, u, :], words[:, u : I // 2 : 2], ident[:])
+            return turned
+
+        def copy_out_scaled_keys(t, turned, tag):
+            ks_in = sb.tile([P, I], BF16, name="ks_in%d" % t, tag=tag, align_bytes=64)
             nc.scalar.copy(
-                ks_in[t // 2][:, (t % 2) * I : (t % 2 + 1) * I].bitcast(F32).rearrange("s (p u) -> s p u", u=2),
+                ks_in[:].bitcast(F32).rearrange("s (p u) -> s p u", u=2),
                 turned[:].rearrange("s u p -> s p u"),
             )
+            return ks_in
 
-        def quantize_scaled_keys(u):
-            ks_scales.append(sb.tile([P, 2 * P], U8, name="ks_scales%d" % u, tag="late%d" % (3 * u), align_bytes=64))
-            nc.vector.quantize_mx(out=ks_codes[u][:].bitcast(FP8X4), scales=ks_scales[u][:], in_=ks_in[u][:])
+        def quantize_scaled_keys(t, ks_in, tag):
+            ks_scales.append(sb.tile([P, P], U8, name="ks_scales%d" % t, tag=tag, align_bytes=64))
+            nc.vector.quantize_mx(out=ks_codes[t][:].bitcast(FP8X4), scales=ks_scales[t][:], in_=ks_in[:])
 
         for t in range(PACK - 1):
             gather(t)
-            scaled_keys(t)
+            turned = scaled_keys(t)
+            if t < 2:
+                quantize_scaled_keys(t, copy_out_scaled_keys(t, turned, "ks_in%d" % t), "ks_scales%d" % t)
             if t == 1:
-                quantize_scaled_keys(0)
                 weave_keys(nc.scalar.copy, 0)
         gather(PACK - 1)
+        last_turned = ps.tile([P, PACK, P], F32, name="last_turned", tag="bank7")
+        for r in range(PACK):
+            nc.tensor.transpose(last_turned[:, r, :], picked[1][:, 1, r:I:PACK], ident[:])
         weave_keys(nc.vector.tensor_copy, 1)
-        nc.vector.quantize_mx(
-            out=key_codes[:].bitcast(FP8X4),
-            scales=key_scales[:],
-            in_=key_bf[:].rearrange("p r s t -> p (r s t)"),
-        )
+
+        def quantize_keys(u):
+            key_scales.append(
+                sb.tile([P, HALF], U8, name="key_scales%d" % u, tag=("key_scales0", "raw3")[u], align_bytes=64)
+            )
+            nc.vector.quantize_mx(
+                out=key_codes[u][:].bitcast(FP8X4),
+                scales=key_scales[u][:],
+                in_=key_bf[:, 2 * u : 2 * u + 2, :, :].rearrange("p r s t -> p (r s t)"),
+            )
 
         cent_codes = sb.tile([P, M], U32, name="cent_codes", align_bytes=64)
         cent_scales = sb.tile([P, M], U8, name="cent_scales", align_bytes=64)
-        cent_all = sb.tile([P, M * PACK], BF16, name="cent_all", tag="stage2", align_bytes=64)
-        for h in range(2):
-            cent_bf = cent_all[:, h * HALF * PACK : (h + 1) * HALF * PACK]
+        cent_all = sb.tile([P, M * PACK], BF16, name="cent_all", tag="stage1", align_bytes=64)
+        for h in range(4):
             nc.scalar.copy(
-                cent_bf.rearrange("p (c j t) -> p c t j", j=4, t=PACK),
+                cent_all[:, h * P * PACK : (h + 1) * P * PACK].rearrange("p (c j t) -> p c t j", j=4, t=PACK),
                 cent_raw[h][:].rearrange("p t (c j) -> p c t j", j=4),
             )
-            cols = slice(h * HALF, (h + 1) * HALF)
-            nc.vector.quantize_mx(out=cent_codes[:, cols].bitcast(FP8X4), scales=cent_scales[:, cols], in_=cent_bf)
+
+        def quantize_cent(m0, m1):
+            nc.vector.quantize_mx(
+                out=cent_codes[:, m0:m1].bitcast(FP8X4),
+                scales=cent_scales[:, m0:m1],
+                in_=cent_all[:, m0 * PACK : m1 * PACK],
+            )
+
+        quantize_cent(0, 2 * P)
+        quantize_keys(0)
+        quantize_cent(2 * P, 3 * P)
+        quantize_cent(3 * P, 4 * P)
+        quantize_keys(1)
+
+        last_in = sb.tile([P, I], BF16, name="last_in", tag="stage1", align_bytes=64)
+        nc.vector.tensor_tensor(
+            last_in[:].rearrange("s (p r) -> s p r", r=PACK),
+            last_turned[:].rearrange("s r p -> s p r"),
+            last_both[:],
+            ALU.mult,
+        )
+
+        ks_in2 = copy_out_scaled_keys(2, turned, "raw2")
 
         neg_max = sb.tile([P, PACK], F32, name="neg_max")
         sums = sb.tile([P, PACK], F32, name="sums")
         inv = sb.tile([P, PACK], F32, name="inv")
-        shares = [sb.tile([P, M], F32, name="shares%d" % r, tag="late%d" % (r if r else 4), align_bytes=64) for r in range(PACK)]
+        shares = [sb.tile([P, M], F32, name="shares%d" % r, tag="shares%d" % r, align_bytes=64) for r in range(PACK)]
         scores = [ps.tile([P, M], F32, name="scores%d" % r, tag="bank%d" % r) for r in range(PACK)]
-        w_pair = sb.tile([P, 2, M, 2], BF16, name="w_pair")
+        w_rows = sb.tile([P, PACK, M], BF16, name="w_rows")
 
         def score(r):
-            cols = slice(r * P, (r + 1) * P)
+            cols = slice(r % 2 * P, (r % 2 + 1) * P)
             nc.tensor.matmul_mx(
                 out=scores[r][:],
-                lhsT=key_codes[:, cols].bitcast(FP8X4),
-                lhsT_scale=key_scales[:, cols],
+                lhsT=key_codes[r // 2][:, cols].bitcast(FP8X4),
+                lhsT_scale=key_scales[r // 2][:, cols],
                 rhs=cent_codes[:].bitcast(FP8X4),
                 rhs_scale=cent_scales[:],
                 start=True,
@@ -154,7 +195,7 @@ def tile_attend_softcluster_kernel(tc, keys, cent, fac, ksc, dsc, offs, out):
 
         def weigh(r, cols):
             nc.vector.tensor_scalar(
-                w_pair[:, r // 2, cols, r % 2],
+                w_rows[:, r, cols],
                 shares[r][:, cols],
                 inv[:, r : r + 1],
                 fac4[:, r : r + 1],
@@ -168,11 +209,23 @@ def tile_attend_softcluster_kernel(tc, keys, cent, fac, ksc, dsc, offs, out):
         invert(0, 1)
         score(3)
         invert(1, 3)
+        warm = ps.tile([P, M], F32, name="warm", tag="bank2")
+        for r in range(2):
+            cols = slice(r % 2 * P, (r % 2 + 1) * P)
+            nc.tensor.matmul_mx(
+                out=warm[:],
+                lhsT=key_codes[r // 2][:, cols].bitcast(FP8X4),
+                lhsT_scale=key_scales[r // 2][:, cols],
+                rhs=cent_codes[:].bitcast(FP8X4),
+                rhs_scale=cent_scales[:],
+                start=True,
+                stop=True,
+            )
         weigh(0, every)
         weigh(1, every)
         invert(3, 4)
-        scaled_keys(PACK - 1)
         weigh(2, every)
+        quantize_scaled_keys(2, ks_in2, "ks_scales2")
         for h in range(2):
             weigh(3, slice(h * HALF, (h + 1) * HALF))
 
@@ -180,13 +233,13 @@ def tile_attend_softcluster_kernel(tc, keys, cent, fac, ksc, dsc, offs, out):
         w_codes = [sb.tile([P, HALF], U32, name="w_codes%d" % h, align_bytes=64) for h in range(2)]
         w_scales = [sb.tile([P, HALF], U8, name="w_scales%d" % h, align_bytes=64) for h in range(2)]
         nc.vector.tensor_copy(
-            w_in[0][:].rearrange("s (m u e) -> s m u e", u=2, e=2),
-            w_pair[:, :, 0:HALF, :].rearrange("s u m e -> s m u e"),
+            w_in[0][:].rearrange("s (c j r) -> s c r j", j=4, r=PACK),
+            w_rows[:, :, 0:HALF].rearrange("s r (c j) -> s c r j", j=4),
         )
-        quantize_scaled_keys(1)
+        quantize_scaled_keys(PACK - 1, last_in, "shares3")
         nc.scalar.copy(
-            w_in[1][:].rearrange("s (m u e) -> s m u e", u=2, e=2),
-            w_pair[:, :, HALF:M, :].rearrange("s u m e -> s m u e"),
+            w_in[1][:].rearrange("s (c j r) -> s c r j", j=4, r=PACK),
+            w_rows[:, :, HALF:M].rearrange("s r (c j) -> s c r j", j=4),
         )
         for h in range(2):
             nc.vector.quantize_mx(out=w_codes[h][:].bitcast(FP8X4), scales=w_scales[h][:], in_=w_in[h][:])
@@ -194,21 +247,20 @@ def tile_attend_softcluster_kernel(tc, keys, cent, fac, ksc, dsc, offs, out):
 
         out_rows = out.rearrange("(p t) m -> p t m", t=PACK)
         for h in range(2):
-            for u in range(2):
-                acc = ps.tile([P, 2, HALF], F32, name="acc%d%d" % (h, u), tag="bank%d" % (2 * h + u))
-                for e in range(2):
-                    nc.tensor.matmul_mx(
-                        out=acc[:, e, :],
-                        lhsT=ks_codes[u][:, e * P : (e + 1) * P].bitcast(FP8X4),
-                        lhsT_scale=ks_scales[u][:, e * P : (e + 1) * P],
-                        rhs=w_codes[h][:].bitcast(FP8X4),
-                        rhs_scale=w_scales[h][:],
-                        start=True,
-                        stop=True,
-                    )
-                res = sb.tile([P, 2, HALF], F32, name="res%d%d" % (h, u))
-                if u == 1:
+            for t in range(PACK):
+                acc = ps.tile([P, HALF], F32, name="acc%d%d" % (h, t), tag="bank%d" % (7 - PACK * h - t))
+                nc.tensor.matmul_mx(
+                    out=acc[:],
+                    lhsT=ks_codes[t][:].bitcast(FP8X4),
+                    lhsT_scale=ks_scales[t][:],
+                    rhs=w_codes[h][:].bitcast(FP8X4),
+                    rhs_scale=w_scales[h][:],
+                    start=True,
+                    stop=True,
+                )
+                res = sb.tile([P, HALF], F32, name="res%d%d" % (h, t))
+                if t % 2 == 1:
                     nc.vector.tensor_copy(res[:], acc[:])
                 else:
                     nc.scalar.copy(res[:], acc[:])
-                nc.sync.dma_start(out=out_rows[:, 2 * u : 2 * u + 2, h * HALF : (h + 1) * HALF], in_=res[:])
+                nc.sync.dma_start(out=out_rows[:, t, h * HALF : (h + 1) * HALF], in_=res[:])

@@ -76,7 +76,7 @@ def tile_attend_softcluster_kernel(tc, keys, cent, fac, ksc, dsc, offs, out):
                 scale=dsc4[:, t : t + 1],
             )
 
-        key_bf = sb.tile([P, PACK, P, PACK], BF16, name="key_bf", align_bytes=64)
+        key_bf = sb.tile([P, PACK, P, PACK], BF16, name="key_bf", tag="key_bf", align_bytes=64)
         key_codes = [sb.tile([P, HALF], U32, name="key_codes%d" % u, align_bytes=64) for u in range(2)]
         key_scales = []
         ks_codes = [sb.tile([P, P], U32, name="ks_codes%d" % t, align_bytes=64) for t in range(PACK)]
@@ -100,23 +100,20 @@ def tile_attend_softcluster_kernel(tc, keys, cent, fac, ksc, dsc, offs, out):
                 nc.tensor.transpose(turned[:, u, :], words[:, u : I // 2 : 2], ident[:])
             return turned
 
-        def copy_out_scaled_keys(t, turned, tag):
-            ks_in = sb.tile([P, I], BF16, name="ks_in%d" % t, tag=tag, align_bytes=64)
-            nc.scalar.copy(
-                ks_in[:].bitcast(F32).rearrange("s (p u) -> s p u", u=2),
-                turned[:].rearrange("s u p -> s p u"),
-            )
-            return ks_in
+        def copy_out_scaled_keys(turned, words):
+            nc.scalar.copy(words.rearrange("s (p u) -> s p u", u=2), turned[:].rearrange("s u p -> s p u"))
+            return words.bitcast(BF16)
 
         def quantize_scaled_keys(t, ks_in, tag):
             ks_scales.append(sb.tile([P, P], U8, name="ks_scales%d" % t, tag=tag, align_bytes=64))
-            nc.vector.quantize_mx(out=ks_codes[t][:].bitcast(FP8X4), scales=ks_scales[t][:], in_=ks_in[:])
+            nc.vector.quantize_mx(out=ks_codes[t][:].bitcast(FP8X4), scales=ks_scales[t][:], in_=ks_in)
 
         for t in range(PACK - 1):
             gather(t)
             turned = scaled_keys(t)
             if t < 2:
-                quantize_scaled_keys(t, copy_out_scaled_keys(t, turned, "ks_in%d" % t), "ks_scales%d" % t)
+                ks_words = sb.tile([P, I // 2], F32, name="ks_words%d" % t, align_bytes=64)
+                quantize_scaled_keys(t, copy_out_scaled_keys(turned, ks_words[:]), "ks_scales%d" % t)
             if t == 1:
                 weave_keys(nc.scalar.copy, 0)
         gather(PACK - 1)
@@ -127,7 +124,7 @@ def tile_attend_softcluster_kernel(tc, keys, cent, fac, ksc, dsc, offs, out):
 
         def quantize_keys(u):
             key_scales.append(
-                sb.tile([P, HALF], U8, name="key_scales%d" % u, tag=("key_scales0", "raw3")[u], align_bytes=64)
+                sb.tile([P, HALF], U8, name="key_scales%d" % u, tag=("key_scales0", "stage1")[u], align_bytes=64)
             )
             nc.vector.quantize_mx(
                 out=key_codes[u][:].bitcast(FP8X4),
@@ -157,15 +154,18 @@ def tile_attend_softcluster_kernel(tc, keys, cent, fac, ksc, dsc, offs, out):
         quantize_cent(3 * P, 4 * P)
         quantize_keys(1)
 
-        last_in = sb.tile([P, I], BF16, name="last_in", tag="stage1", align_bytes=64)
-        nc.vector.tensor_tensor(
-            last_in[:].rearrange("s (p r) -> s p r", r=PACK),
-            last_turned[:].rearrange("s r p -> s p r"),
-            last_both[:],
+        late = sb.tile([P, I + I // 2], F32, name="late", tag="raw3", align_bytes=64)
+        last_keys = late[:, 0:I]
+        nc.scalar.copy(last_keys.rearrange("s (p r) -> s p r", r=PACK), last_turned[:].rearrange("s r p -> s p r"))
+        last_in = sb.tile([P, I], BF16, name="last_in", tag="key_bf", align_bytes=64)
+        nc.gpsimd.tensor_tensor(
+            last_in[:],
+            last_keys,
+            last_both[:].rearrange("s p r -> s (p r)"),
             ALU.mult,
         )
 
-        ks_in2 = copy_out_scaled_keys(2, turned, "raw2")
+        ks_in2 = copy_out_scaled_keys(turned, late[:, I : I + I // 2])
 
         neg_max = sb.tile([P, PACK], F32, name="neg_max")
         sums = sb.tile([P, PACK], F32, name="sums")
@@ -176,15 +176,16 @@ def tile_attend_softcluster_kernel(tc, keys, cent, fac, ksc, dsc, offs, out):
 
         def score(r):
             cols = slice(r % 2 * P, (r % 2 + 1) * P)
-            nc.tensor.matmul_mx(
-                out=scores[r][:],
-                lhsT=key_codes[r // 2][:, cols].bitcast(FP8X4),
-                lhsT_scale=key_scales[r // 2][:, cols],
-                rhs=cent_codes[:].bitcast(FP8X4),
-                rhs_scale=cent_scales[:],
-                start=True,
-                stop=True,
-            )
+            for m0, m1 in ((0, 2 * P), (2 * P, 3 * P), (3 * P, M)) if r == 0 else ((0, M),):
+                nc.tensor.matmul_mx(
+                    out=scores[r][:, m0:m1],
+                    lhsT=key_codes[r // 2][:, cols].bitcast(FP8X4),
+                    lhsT_scale=key_scales[r // 2][:, cols],
+                    rhs=cent_codes[:, m0:m1].bitcast(FP8X4),
+                    rhs_scale=cent_scales[:, m0:m1],
+                    start=True,
+                    stop=True,
+                )
             nc.vector.tensor_reduce(neg_max[:, r : r + 1], scores[r][:], AXIS.X, ALU.max, negate=True)
             nc.scalar.activation(
                 shares[r][:], scores[r][:], ACT.Exp, bias=neg_max[:, r : r + 1], accum_out=sums[:, r : r + 1]
@@ -193,8 +194,8 @@ def tile_attend_softcluster_kernel(tc, keys, cent, fac, ksc, dsc, offs, out):
         def invert(r0, r1):
             nc.vector.reciprocal(inv[:, r0:r1], sums[:, r0:r1])
 
-        def weigh(r, cols):
-            nc.vector.tensor_scalar(
+        def weigh(r, cols, engine=nc.vector):
+            engine.tensor_scalar(
                 w_rows[:, r, cols],
                 shares[r][:, cols],
                 inv[:, r : r + 1],
@@ -209,7 +210,7 @@ def tile_attend_softcluster_kernel(tc, keys, cent, fac, ksc, dsc, offs, out):
         invert(0, 1)
         score(3)
         invert(1, 3)
-        warm = ps.tile([P, M], F32, name="warm", tag="bank2")
+        warm = ps.tile([P, M], F32, name="warm", tag="bank3")
         for r in range(2):
             cols = slice(r % 2 * P, (r % 2 + 1) * P)
             nc.tensor.matmul_mx(
@@ -221,11 +222,14 @@ def tile_attend_softcluster_kernel(tc, keys, cent, fac, ksc, dsc, offs, out):
                 start=True,
                 stop=True,
             )
-        weigh(0, every)
-        weigh(1, every)
-        invert(3, 4)
+        weigh(0, every, nc.gpsimd)
+        factor1 = sb.tile([P, 1], F32, name="factor1")
+        nc.vector.tensor_tensor(factor1[:], inv[:, 1:2], fac4[:, 1:2], ALU.mult)
+        nc.scalar.activation(w_rows[:, 1, :], shares[1][:], ACT.Copy, scale=factor1[:])
         weigh(2, every)
         quantize_scaled_keys(2, ks_in2, "ks_scales2")
+        invert(3, 4)
+        quantize_scaled_keys(PACK - 1, last_in[:], "shares2")
         for h in range(2):
             weigh(3, slice(h * HALF, (h + 1) * HALF))
 
@@ -236,7 +240,6 @@ def tile_attend_softcluster_kernel(tc, keys, cent, fac, ksc, dsc, offs, out):
             w_in[0][:].rearrange("s (c j r) -> s c r j", j=4, r=PACK),
             w_rows[:, :, 0:HALF].rearrange("s r (c j) -> s c r j", j=4),
         )
-        quantize_scaled_keys(PACK - 1, last_in, "shares3")
         nc.scalar.copy(
             w_in[1][:].rearrange("s (c j r) -> s c r j", j=4, r=PACK),
             w_rows[:, :, HALF:M].rearrange("s r (c j) -> s c r j", j=4),

@@ -210,18 +210,6 @@ def tile_attend_softcluster_kernel(tc, keys, cent, fac, ksc, dsc, offs, out):
         invert(0, 1)
         score(3)
         invert(1, 3)
-        warm = ps.tile([P, M], F32, name="warm", tag="bank3")
-        for r in range(2):
-            cols = slice(r % 2 * P, (r % 2 + 1) * P)
-            nc.tensor.matmul_mx(
-                out=warm[:],
-                lhsT=key_codes[r // 2][:, cols].bitcast(FP8X4),
-                lhsT_scale=key_scales[r // 2][:, cols],
-                rhs=cent_codes[:].bitcast(FP8X4),
-                rhs_scale=cent_scales[:],
-                start=True,
-                stop=True,
-            )
         weigh(0, every, nc.gpsimd)
         factor1 = sb.tile([P, 1], F32, name="factor1")
         nc.vector.tensor_tensor(factor1[:], inv[:, 1:2], fac4[:, 1:2], ALU.mult)
@@ -250,20 +238,26 @@ def tile_attend_softcluster_kernel(tc, keys, cent, fac, ksc, dsc, offs, out):
 
         out_rows = out.rearrange("(p t) m -> p t m", t=PACK)
         for h in range(2):
-            for t in range(PACK):
-                acc = ps.tile([P, HALF], F32, name="acc%d%d" % (h, t), tag="bank%d" % (7 - PACK * h - t))
-                nc.tensor.matmul_mx(
-                    out=acc[:],
-                    lhsT=ks_codes[t][:].bitcast(FP8X4),
-                    lhsT_scale=ks_scales[t][:],
-                    rhs=w_codes[h][:].bitcast(FP8X4),
-                    rhs_scale=w_scales[h][:],
-                    start=True,
-                    stop=True,
-                )
-                res = sb.tile([P, HALF], F32, name="res%d%d" % (h, t))
-                if t % 2 == 1:
-                    nc.vector.tensor_copy(res[:], acc[:])
-                else:
-                    nc.scalar.copy(res[:], acc[:])
-                nc.sync.dma_start(out=out_rows[:, t, h * HALF : (h + 1) * HALF], in_=res[:])
+            for t0 in range(0, PACK, 2):
+                res = sb.tile([P, 2, HALF], F32, name="res%d%d" % (h, t0))
+                cols = slice(h * HALF, (h + 1) * HALF)
+                for e in range(2):
+                    t = t0 + e
+                    acc = ps.tile([P, HALF], F32, name="acc%d%d" % (h, t), tag="bank%d" % (7 - PACK * h - t))
+                    nc.tensor.matmul_mx(
+                        out=acc[:],
+                        lhsT=ks_codes[t][:].bitcast(FP8X4),
+                        lhsT_scale=ks_scales[t][:],
+                        rhs=w_codes[h][:].bitcast(FP8X4),
+                        rhs_scale=w_scales[h][:],
+                        start=True,
+                        stop=True,
+                    )
+                    if e == 1:
+                        nc.vector.tensor_copy(res[:, e, :], acc[:])
+                    else:
+                        nc.scalar.copy(res[:, e, :], acc[:])
+                    if h == 0 and t0 == 0:
+                        nc.sync.dma_start(out=out_rows[:, t, cols], in_=res[:, e, :])
+                if h > 0 or t0 > 0:
+                    nc.sync.dma_start(out=out_rows[:, t0 : t0 + 2, cols], in_=res[:])

@@ -18,7 +18,31 @@ AXIS = mybir.AxisListType
 
 P = 128
 PACK = 4
+LAST = PACK - 1
 HALF = M // 2
+PIECES = 4
+PIECE = M // PIECES
+RUN = 4
+ALIGN = 64
+
+
+def mx_product(nc, acc, lhs_codes, lhs_scales, rhs_codes, rhs_scales):
+    nc.tensor.matmul_mx(
+        out=acc,
+        lhsT=lhs_codes.bitcast(FP8X4),
+        lhsT_scale=lhs_scales,
+        rhs=rhs_codes.bitcast(FP8X4),
+        rhs_scale=rhs_scales,
+        start=True,
+        stop=True,
+    )
+
+
+def weave(copy, woven, rows):
+    copy(
+        woven.rearrange("p (c j k) -> p c k j", j=RUN, k=PACK),
+        rows.rearrange("p k (c j) -> p c k j", j=RUN),
+    )
 
 
 def tile_attend_softcluster_kernel(tc, keys, cent, fac, ksc, dsc, offs, out):
@@ -28,236 +52,216 @@ def tile_attend_softcluster_kernel(tc, keys, cent, fac, ksc, dsc, offs, out):
         ps = ctx.enter_context(tc.psum_pool(name="ps", bufs=1))
 
         offsets = sb.tile([P, I // 16], U16, name="offsets")
-
         key_rows = keys.rearrange("(p t) n -> p t n", t=PACK)
-        pool_t = [sb.tile([P, T], F32, name="pool%d" % t) for t in range(PACK)]
-        nc.sync.dma_start(out=pool_t[0][:], in_=key_rows[:, 0, :])
+        planes = [sb.tile([P, T], F32, name="plane%d" % t) for t in range(PACK)]
         nc.sync.dma_start(offsets[:], offs)
-        ksc4 = sb.tile([P, PACK], F32, name="ksc4")
+        nc.sync.dma_start(out=planes[0][:], in_=key_rows[:, 0, :])
+        picked = [sb.tile([P, 2, I], F32, name="picked%d" % u) for u in range(2)]
+        ksc4 = picked[0][:, 0, 0:PACK]
         dsc4 = sb.tile([P, PACK], F32, name="dsc4")
         fac4 = sb.tile([P, PACK], F32, name="fac4")
-        nc.scalar.dma_start(out=ksc4[:], in_=ksc.rearrange("(s r) o -> s (r o)", r=PACK))
+        nc.scalar.dma_start(out=ksc4, in_=ksc.rearrange("(s r) o -> s (r o)", r=PACK))
         nc.scalar.dma_start(out=dsc4[:], in_=dsc.rearrange("o (p t) -> p (o t)", t=PACK))
         for t in range(1, PACK):
-            nc.sync.dma_start(out=pool_t[t][:], in_=key_rows[:, t, :])
+            nc.sync.dma_start(out=planes[t][:], in_=key_rows[:, t, :])
         cent_rows = cent.rearrange("(p t) m -> p t m", t=PACK)
-        cent_raw = [sb.tile([P, PACK, P], F32, name="cent_raw%d" % h, tag="raw%d" % h, align_bytes=64) for h in range(4)]
-        for h in range(4):
-            nc.sync.dma_start(out=cent_raw[h][:], in_=cent_rows[:, :, h * P : (h + 1) * P])
+        cent_raw = [
+            sb.tile([P, PACK, PIECE], F32, name="cent_raw%d" % c, tag="cent_raw%d" % c, align_bytes=ALIGN)
+            for c in range(PIECES)
+        ]
+        for c in range(PIECES):
+            nc.sync.dma_start(out=cent_raw[c][:], in_=cent_rows[:, :, c * PIECE : (c + 1) * PIECE])
         nc.sync.dma_start(out=fac4[:], in_=fac.rearrange("(s r) o -> s (r o)", r=PACK))
-
-        warm_in = sb.tile([P, 1], F32, name="warm_in")
-        warm_out = sb.tile([P, 1], F32, name="warm_out")
-        nc.vector.memset(warm_in[:], 0.0)
-        nc.scalar.activation(warm_out[:], warm_in[:], ACT.Exp)
 
         ident = sb.tile([P, P], F32, name="ident")
         make_identity(nc, ident[:])
 
+        exp_preload = sb.tile([P, 1], F32, name="exp_preload")
+        nc.scalar.activation(exp_preload[:], ident[:, 0:1], ACT.Exp)
+
         ksc_bank = ps.tile([P, PACK, P], F32, name="ksc_bank", tag="bank4")
         for r in range(PACK):
             nc.tensor.transpose(ksc_bank[:, r, :], ksc4[:, r : r + 1].to_broadcast([P, P]), ident[:])
-        picked = [sb.tile([P, 2, I], F32, name="picked%d" % u) for u in range(2)]
-        both = [picked[(t + 1) // 2][:, (t + 1) % 2, :] for t in range(PACK - 1)]
+        tables = [picked[(t + 1) // 2][:, (t + 1) % 2, :] for t in range(LAST)]
         dsc_bank = ps.tile([P, P], F32, name="dsc_bank", tag="bank7")
-        nc.tensor.transpose(dsc_bank[:], dsc4[:, PACK - 1 : PACK].to_broadcast([P, P]), ident[:])
-        last_both = sb.tile([P, P, PACK], F32, name="last_both")
+        nc.tensor.transpose(dsc_bank[:], dsc4[:, LAST:PACK].to_broadcast([P, P]), ident[:])
+        last_table = sb.tile([P, P, PACK], F32, name="last_table")
         nc.vector.tensor_tensor(
-            last_both[:],
+            last_table[:],
             dsc_bank[:].unsqueeze(2).to_broadcast([P, P, PACK]),
-            ksc4[:].unsqueeze(1).to_broadcast([P, P, PACK]),
+            ksc4.unsqueeze(1).to_broadcast([P, P, PACK]),
             ALU.mult,
         )
-        for t in range(PACK - 1):
+        for t in range(LAST):
             nc.scalar.activation(
-                both[t].rearrange("p (s r) -> p s r", r=PACK),
+                tables[t].rearrange("p (s r) -> p s r", r=PACK),
                 ksc_bank[:].rearrange("p r s -> p s r"),
                 ACT.Copy,
                 scale=dsc4[:, t : t + 1],
             )
 
-        key_bf = sb.tile([P, PACK, P, PACK], BF16, name="key_bf", tag="key_bf", align_bytes=64)
-        key_codes = [sb.tile([P, HALF], U32, name="key_codes%d" % u, align_bytes=64) for u in range(2)]
+        key_bf = sb.tile([P, PACK, P, PACK], BF16, name="key_bf", tag="key_bf", align_bytes=ALIGN)
+        key_codes = [sb.tile([P, 2 * P], U32, name="key_codes%d" % u, align_bytes=ALIGN) for u in range(2)]
         key_scales = []
-        ks_codes = [sb.tile([P, P], U32, name="ks_codes%d" % t, align_bytes=64) for t in range(PACK)]
+        ks_codes = [sb.tile([P, P], U32, name="ks_codes%d" % t, align_bytes=ALIGN) for t in range(PACK)]
         ks_scales = []
 
         def gather(t):
-            nc.vector.tensor_copy(picked[t // 2][:, t % 2, :], pool_t[t][:].indirect(offsets[:]))
+            nc.vector.tensor_copy(picked[t // 2][:, t % 2, :], planes[t][:].indirect(offsets[:]))
 
-        def weave_keys(copy, u):
+        def weave_key_planes(copy, u):
             copy(
                 key_bf[:, :, :, 2 * u : 2 * u + 2].rearrange("p r s e -> p s e r"),
                 picked[u][:].rearrange("p e (s r) -> p s e r", r=PACK),
             )
 
-        def scaled_keys(t):
-            ks_bf = sb.tile([P, I], BF16, name="ks_bf%d" % t, tag="stage%d" % t, align_bytes=64)
-            nc.vector.tensor_tensor(ks_bf[:], picked[t // 2][:, t % 2, :], both[t], ALU.mult)
-            words = ks_bf[:].bitcast(F32)
+        def scale_and_turn(t):
+            ks_bf = sb.tile([P, I], BF16, name="ks_bf%d" % t, tag="ks_bf%d" % t, align_bytes=ALIGN)
+            nc.vector.tensor_tensor(ks_bf[:], picked[t // 2][:, t % 2, :], tables[t], ALU.mult)
+            pairs = ks_bf[:].bitcast(F32)
             turned = ps.tile([P, 2, P], F32, name="turned%d" % t, tag="bank%d" % (5 + t % 2))
             for u in range(2):
-                nc.tensor.transpose(turned[:, u, :], words[:, u : I // 2 : 2], ident[:])
+                nc.tensor.transpose(turned[:, u, :], pairs[:, u : I // 2 : 2], ident[:])
             return turned
 
-        def copy_out_scaled_keys(turned, words):
-            nc.scalar.copy(words.rearrange("s (p u) -> s p u", u=2), turned[:].rearrange("s u p -> s p u"))
-            return words.bitcast(BF16)
+        def weave_turned(turned, pairs):
+            nc.scalar.copy(pairs.rearrange("s (p u) -> s p u", u=2), turned[:].rearrange("s u p -> s p u"))
+            return pairs.bitcast(BF16)
 
-        def quantize_scaled_keys(t, ks_in, tag):
-            ks_scales.append(sb.tile([P, P], U8, name="ks_scales%d" % t, tag=tag, align_bytes=64))
+        def quantize_ks(t, ks_in, scales_tag):
+            ks_scales.append(sb.tile([P, P], U8, name="ks_scales%d" % t, tag=scales_tag, align_bytes=ALIGN))
             nc.vector.quantize_mx(out=ks_codes[t][:].bitcast(FP8X4), scales=ks_scales[t][:], in_=ks_in)
 
-        for t in range(PACK - 1):
+        for t in range(2):
             gather(t)
-            turned = scaled_keys(t)
-            if t < 2:
-                ks_words = sb.tile([P, I // 2], F32, name="ks_words%d" % t, align_bytes=64)
-                quantize_scaled_keys(t, copy_out_scaled_keys(turned, ks_words[:]), "ks_scales%d" % t)
-            if t == 1:
-                weave_keys(nc.scalar.copy, 0)
-        gather(PACK - 1)
+            turned = scale_and_turn(t)
+            ks_pairs = sb.tile([P, I // 2], F32, name="ks_pairs%d" % t, align_bytes=ALIGN)
+            quantize_ks(t, weave_turned(turned, ks_pairs[:]), "ks_scales%d" % t)
+        weave_key_planes(nc.scalar.copy, 0)
+        gather(2)
+        turned2 = scale_and_turn(2)
+        gather(LAST)
         last_turned = ps.tile([P, PACK, P], F32, name="last_turned", tag="bank7")
         for r in range(PACK):
             nc.tensor.transpose(last_turned[:, r, :], picked[1][:, 1, r:I:PACK], ident[:])
-        weave_keys(nc.vector.tensor_copy, 1)
+        weave_key_planes(nc.vector.tensor_copy, 1)
 
-        def quantize_keys(u):
-            key_scales.append(
-                sb.tile([P, HALF], U8, name="key_scales%d" % u, tag=("key_scales0", "stage1")[u], align_bytes=64)
-            )
+        def quantize_keys(u, scales_tag):
+            key_scales.append(sb.tile([P, 2 * P], U8, name="key_scales%d" % u, tag=scales_tag, align_bytes=ALIGN))
             nc.vector.quantize_mx(
                 out=key_codes[u][:].bitcast(FP8X4),
                 scales=key_scales[u][:],
                 in_=key_bf[:, 2 * u : 2 * u + 2, :, :].rearrange("p r s t -> p (r s t)"),
             )
 
-        cent_codes = sb.tile([P, M], U32, name="cent_codes", align_bytes=64)
-        cent_scales = sb.tile([P, M], U8, name="cent_scales", align_bytes=64)
-        cent_all = sb.tile([P, M * PACK], BF16, name="cent_all", tag="stage1", align_bytes=64)
-        for h in range(4):
-            nc.scalar.copy(
-                cent_all[:, h * P * PACK : (h + 1) * P * PACK].rearrange("p (c j t) -> p c t j", j=4, t=PACK),
-                cent_raw[h][:].rearrange("p t (c j) -> p c t j", j=4),
-            )
+        cent_codes = sb.tile([P, M], U32, name="cent_codes", align_bytes=ALIGN)
+        cent_scales = sb.tile([P, M], U8, name="cent_scales", align_bytes=ALIGN)
+        cent_bf = sb.tile([P, M * PACK], BF16, name="cent_bf", tag="ks_bf1", align_bytes=ALIGN)
+        for c in range(PIECES):
+            weave(nc.scalar.copy, cent_bf[:, c * PIECE * PACK : (c + 1) * PIECE * PACK], cent_raw[c][:])
 
         def quantize_cent(m0, m1):
             nc.vector.quantize_mx(
                 out=cent_codes[:, m0:m1].bitcast(FP8X4),
                 scales=cent_scales[:, m0:m1],
-                in_=cent_all[:, m0 * PACK : m1 * PACK],
+                in_=cent_bf[:, m0 * PACK : m1 * PACK],
             )
 
-        quantize_cent(0, 2 * P)
-        quantize_keys(0)
-        quantize_cent(2 * P, 3 * P)
-        quantize_cent(3 * P, 4 * P)
-        quantize_keys(1)
+        cent_spans = ((0, 2 * PIECE), (2 * PIECE, 3 * PIECE), (3 * PIECE, M))
+        quantize_cent(*cent_spans[0])
+        quantize_keys(0, "key_scales0")
+        quantize_cent(*cent_spans[1])
+        quantize_cent(*cent_spans[2])
+        quantize_keys(1, "ks_bf1")
 
-        late = sb.tile([P, I + I // 2], F32, name="late", tag="raw3", align_bytes=64)
+        late = sb.tile([P, I + I // 2], F32, name="late", tag="cent_raw%d" % (PIECES - 1), align_bytes=ALIGN)
         last_keys = late[:, 0:I]
         nc.scalar.copy(last_keys.rearrange("s (p r) -> s p r", r=PACK), last_turned[:].rearrange("s r p -> s p r"))
-        last_in = sb.tile([P, I], BF16, name="last_in", tag="key_bf", align_bytes=64)
-        nc.gpsimd.tensor_tensor(
-            last_in[:],
-            last_keys,
-            last_both[:].rearrange("s p r -> s (p r)"),
-            ALU.mult,
-        )
-
-        ks_in2 = copy_out_scaled_keys(turned, late[:, I : I + I // 2])
+        last_ks = sb.tile([P, I], BF16, name="last_ks", tag="key_bf", align_bytes=ALIGN)
+        nc.gpsimd.tensor_tensor(last_ks[:], last_keys, last_table[:].rearrange("s p r -> s (p r)"), ALU.mult)
+        ks_in2 = weave_turned(turned2, late[:, I : I + I // 2])
 
         neg_max = sb.tile([P, PACK], F32, name="neg_max")
         sums = sb.tile([P, PACK], F32, name="sums")
-        inv = sb.tile([P, PACK], F32, name="inv")
-        shares = [sb.tile([P, M], F32, name="shares%d" % r, tag="shares%d" % r, align_bytes=64) for r in range(PACK)]
+        inv_sums = sb.tile([P, PACK], F32, name="inv_sums")
+        exps = [sb.tile([P, M], F32, name="exps%d" % r, tag="exps%d" % r, align_bytes=ALIGN) for r in range(PACK)]
         scores = [ps.tile([P, M], F32, name="scores%d" % r, tag="bank%d" % r) for r in range(PACK)]
         w_rows = sb.tile([P, PACK, M], BF16, name="w_rows")
 
-        def score(r):
+        def score_product(acc, r, m0, m1):
             cols = slice(r % 2 * P, (r % 2 + 1) * P)
-            for m0, m1 in ((0, 2 * P), (2 * P, 3 * P), (3 * P, M)) if r == 0 else ((0, M),):
-                nc.tensor.matmul_mx(
-                    out=scores[r][:, m0:m1],
-                    lhsT=key_codes[r // 2][:, cols].bitcast(FP8X4),
-                    lhsT_scale=key_scales[r // 2][:, cols],
-                    rhs=cent_codes[:, m0:m1].bitcast(FP8X4),
-                    rhs_scale=cent_scales[:, m0:m1],
-                    start=True,
-                    stop=True,
-                )
+            mx_product(
+                nc,
+                acc[:, m0:m1],
+                key_codes[r // 2][:, cols],
+                key_scales[r // 2][:, cols],
+                cent_codes[:, m0:m1],
+                cent_scales[:, m0:m1],
+            )
+
+        def softmax_terms(r):
+            for m0, m1 in cent_spans if r == 0 else ((0, M),):
+                score_product(scores[r], r, m0, m1)
             nc.vector.tensor_reduce(neg_max[:, r : r + 1], scores[r][:], AXIS.X, ALU.max, negate=True)
             nc.scalar.activation(
-                shares[r][:], scores[r][:], ACT.Exp, bias=neg_max[:, r : r + 1], accum_out=sums[:, r : r + 1]
+                exps[r][:], scores[r][:], ACT.Exp, bias=neg_max[:, r : r + 1], accum_out=sums[:, r : r + 1]
             )
 
         def invert(r0, r1):
-            nc.vector.reciprocal(inv[:, r0:r1], sums[:, r0:r1])
+            nc.vector.reciprocal(inv_sums[:, r0:r1], sums[:, r0:r1])
 
-        def weigh(r, cols, engine=nc.vector):
+        def weigh(engine, r, m0, m1):
             engine.tensor_scalar(
-                w_rows[:, r, cols],
-                shares[r][:, cols],
-                inv[:, r : r + 1],
+                w_rows[:, r, m0:m1],
+                exps[r][:, m0:m1],
+                inv_sums[:, r : r + 1],
                 fac4[:, r : r + 1],
                 ALU.mult,
                 ALU.mult,
             )
 
-        every = slice(0, M)
-        for r in range(3):
-            score(r)
+        for r in range(LAST):
+            softmax_terms(r)
         invert(0, 1)
-        score(3)
-        invert(1, 3)
-        weigh(0, every, nc.gpsimd)
-        factor1 = sb.tile([P, 1], F32, name="factor1")
-        nc.vector.tensor_tensor(factor1[:], inv[:, 1:2], fac4[:, 1:2], ALU.mult)
-        nc.scalar.activation(w_rows[:, 1, :], shares[1][:], ACT.Copy, scale=factor1[:])
-        weigh(2, every)
-        quantize_scaled_keys(2, ks_in2, "ks_scales2")
-        invert(3, 4)
-        quantize_scaled_keys(PACK - 1, last_in[:], "shares2")
-        for h in range(2):
-            weigh(3, slice(h * HALF, (h + 1) * HALF))
+        softmax_terms(LAST)
+        invert(1, LAST)
 
-        w_in = [sb.tile([P, HALF * PACK], BF16, name="w_in%d" % h, align_bytes=64) for h in range(2)]
-        w_codes = [sb.tile([P, HALF], U32, name="w_codes%d" % h, align_bytes=64) for h in range(2)]
-        w_scales = [sb.tile([P, HALF], U8, name="w_scales%d" % h, align_bytes=64) for h in range(2)]
-        nc.vector.tensor_copy(
-            w_in[0][:].rearrange("s (c j r) -> s c r j", j=4, r=PACK),
-            w_rows[:, :, 0:HALF].rearrange("s r (c j) -> s c r j", j=4),
-        )
-        nc.scalar.copy(
-            w_in[1][:].rearrange("s (c j r) -> s c r j", j=4, r=PACK),
-            w_rows[:, :, HALF:M].rearrange("s r (c j) -> s c r j", j=4),
-        )
+        warm_up = ps.tile([P, M], F32, name="warm_up", tag="bank%d" % LAST)
+        for r in range(2):
+            score_product(warm_up, r, 0, M)
+
+        weigh(nc.gpsimd, 0, 0, M)
+        factor1 = sb.tile([P, 1], F32, name="factor1")
+        nc.vector.tensor_tensor(factor1[:], inv_sums[:, 1:2], fac4[:, 1:2], ALU.mult)
+        nc.scalar.activation(w_rows[:, 1, :], exps[1][:], ACT.Copy, scale=factor1[:])
+        weigh(nc.vector, 2, 0, M)
+        quantize_ks(2, ks_in2, "ks_scales2")
+        invert(LAST, PACK)
+        quantize_ks(LAST, last_ks[:], "exps2")
+        for h in range(2):
+            weigh(nc.vector, LAST, h * HALF, (h + 1) * HALF)
+
+        w_in = [sb.tile([P, HALF * PACK], BF16, name="w_in%d" % h, align_bytes=ALIGN) for h in range(2)]
+        w_codes = [sb.tile([P, HALF], U32, name="w_codes%d" % h, align_bytes=ALIGN) for h in range(2)]
+        w_scales = [sb.tile([P, HALF], U8, name="w_scales%d" % h, align_bytes=ALIGN) for h in range(2)]
+        weave(nc.vector.tensor_copy, w_in[0][:], w_rows[:, :, 0:HALF])
+        weave(nc.scalar.copy, w_in[1][:], w_rows[:, :, HALF:M])
         for h in range(2):
             nc.vector.quantize_mx(out=w_codes[h][:].bitcast(FP8X4), scales=w_scales[h][:], in_=w_in[h][:])
 
-
         out_rows = out.rearrange("(p t) m -> p t m", t=PACK)
+        copies = (nc.scalar.copy, nc.vector.tensor_copy)
         for h in range(2):
+            cols = slice(h * HALF, (h + 1) * HALF)
             for t0 in range(0, PACK, 2):
+                first_pair = h == 0 and t0 == 0
                 res = sb.tile([P, 2, HALF], F32, name="res%d%d" % (h, t0))
-                cols = slice(h * HALF, (h + 1) * HALF)
                 for e in range(2):
                     t = t0 + e
                     acc = ps.tile([P, HALF], F32, name="acc%d%d" % (h, t), tag="bank%d" % (7 - PACK * h - t))
-                    nc.tensor.matmul_mx(
-                        out=acc[:],
-                        lhsT=ks_codes[t][:].bitcast(FP8X4),
-                        lhsT_scale=ks_scales[t][:],
-                        rhs=w_codes[h][:].bitcast(FP8X4),
-                        rhs_scale=w_scales[h][:],
-                        start=True,
-                        stop=True,
-                    )
-                    if e == 1:
-                        nc.vector.tensor_copy(res[:, e, :], acc[:])
-                    else:
-                        nc.scalar.copy(res[:, e, :], acc[:])
-                    if h == 0 and t0 == 0:
+                    mx_product(nc, acc[:], ks_codes[t][:], ks_scales[t][:], w_codes[h][:], w_scales[h][:])
+                    copies[e](res[:, e, :], acc[:])
+                    if first_pair:
                         nc.sync.dma_start(out=out_rows[:, t, cols], in_=res[:, e, :])
-                if h > 0 or t0 > 0:
+                if not first_pair:
                     nc.sync.dma_start(out=out_rows[:, t0 : t0 + 2, cols], in_=res[:])

from contextlib import ExitStack

import concourse.mybir as mybir
from concourse.masks import make_identity

D, T, I, M = 512, 2048, 512, 512
FLOPS = 2 * D * I * M * 2

F32 = mybir.dt.float32
BF16 = mybir.dt.bfloat16
U32 = mybir.dt.uint32
U16 = mybir.dt.uint16
U8 = mybir.dt.uint8
FP8X4 = mybir.dt.float8_e4m3fn_x4
ACT = mybir.ActivationFunctionType
ALU = mybir.AluOpType
AXIS = mybir.AxisListType

P = 128
PACK = 4
LAST = PACK - 1
HALF = M // 2
PIECES = 4
PIECE = M // PIECES
RUN = 4
ALIGN = 64


def mx_product(nc, acc, lhs_codes, lhs_scales, rhs_codes, rhs_scales):
    nc.tensor.matmul_mx(
        out=acc,
        lhsT=lhs_codes.bitcast(FP8X4),
        lhsT_scale=lhs_scales,
        rhs=rhs_codes.bitcast(FP8X4),
        rhs_scale=rhs_scales,
        start=True,
        stop=True,
    )


def weave(copy, woven, rows):
    copy(
        woven.rearrange("p (c j k) -> p c k j", j=RUN, k=PACK),
        rows.rearrange("p k (c j) -> p c k j", j=RUN),
    )


def tile_attend_softcluster_kernel(tc, keys, cent, fac, ksc, dsc, offs, out):
    nc = tc.nc
    with ExitStack() as ctx:
        sb = ctx.enter_context(tc.tile_pool(name="sb", bufs=1))
        ps = ctx.enter_context(tc.psum_pool(name="ps", bufs=1))

        offsets = sb.tile([P, I // 16], U16, name="offsets")
        key_rows = keys.rearrange("(p t) n -> p t n", t=PACK)
        planes = [sb.tile([P, T], F32, name="plane%d" % t) for t in range(PACK)]
        nc.sync.dma_start(offsets[:], offs)
        nc.sync.dma_start(out=planes[0][:], in_=key_rows[:, 0, :])
        picked = [sb.tile([P, 2, I], F32, name="picked%d" % u) for u in range(2)]
        ksc4 = picked[0][:, 0, 0:PACK]
        dsc4 = sb.tile([P, PACK], F32, name="dsc4")
        fac4 = sb.tile([P, PACK], F32, name="fac4")
        nc.scalar.dma_start(out=ksc4, in_=ksc.rearrange("(s r) o -> s (r o)", r=PACK))
        nc.scalar.dma_start(out=dsc4[:], in_=dsc.rearrange("o (p t) -> p (o t)", t=PACK))
        for t in range(1, PACK):
            nc.sync.dma_start(out=planes[t][:], in_=key_rows[:, t, :])
        cent_rows = cent.rearrange("(p t) m -> p t m", t=PACK)
        cent_raw = [
            sb.tile([P, PACK, PIECE], F32, name="cent_raw%d" % c, tag="cent_raw%d" % c, align_bytes=ALIGN)
            for c in range(PIECES)
        ]
        for c in range(PIECES):
            nc.sync.dma_start(out=cent_raw[c][:], in_=cent_rows[:, :, c * PIECE : (c + 1) * PIECE])
        nc.sync.dma_start(out=fac4[:], in_=fac.rearrange("(s r) o -> s (r o)", r=PACK))

        ident = sb.tile([P, P], F32, name="ident")
        make_identity(nc, ident[:])

        exp_preload = sb.tile([P, 1], F32, name="exp_preload")
        nc.scalar.activation(exp_preload[:], ident[:, 0:1], ACT.Exp)

        ksc_bank = ps.tile([P, PACK, P], F32, name="ksc_bank", tag="bank4")
        for r in range(PACK):
            nc.tensor.transpose(ksc_bank[:, r, :], ksc4[:, r : r + 1].to_broadcast([P, P]), ident[:])
        tables = [picked[(t + 1) // 2][:, (t + 1) % 2, :] for t in range(LAST)]
        dsc_bank = ps.tile([P, P], F32, name="dsc_bank", tag="bank7")
        nc.tensor.transpose(dsc_bank[:], dsc4[:, LAST:PACK].to_broadcast([P, P]), ident[:])
        last_table = sb.tile([P, P, PACK], F32, name="last_table")
        nc.vector.tensor_tensor(
            last_table[:],
            dsc_bank[:].unsqueeze(2).to_broadcast([P, P, PACK]),
            ksc4.unsqueeze(1).to_broadcast([P, P, PACK]),
            ALU.mult,
        )
        for t in range(LAST):
            nc.scalar.activation(
                tables[t].rearrange("p (s r) -> p s r", r=PACK),
                ksc_bank[:].rearrange("p r s -> p s r"),
                ACT.Copy,
                scale=dsc4[:, t : t + 1],
            )

        key_bf = sb.tile([P, PACK, P, PACK], BF16, name="key_bf", tag="key_bf", align_bytes=ALIGN)
        key_codes = [sb.tile([P, 2 * P], U32, name="key_codes%d" % u, align_bytes=ALIGN) for u in range(2)]
        key_scales = []
        ks_codes = [sb.tile([P, P], U32, name="ks_codes%d" % t, align_bytes=ALIGN) for t in range(PACK)]
        ks_scales = []

        def gather(t):
            nc.vector.tensor_copy(picked[t // 2][:, t % 2, :], planes[t][:].indirect(offsets[:]))

        def weave_key_planes(copy, u):
            copy(
                key_bf[:, :, :, 2 * u : 2 * u + 2].rearrange("p r s e -> p s e r"),
                picked[u][:].rearrange("p e (s r) -> p s e r", r=PACK),
            )

        def scale_and_turn(t):
            ks_bf = sb.tile([P, I], BF16, name="ks_bf%d" % t, tag="ks_bf%d" % t, align_bytes=ALIGN)
            nc.vector.tensor_tensor(ks_bf[:], picked[t // 2][:, t % 2, :], tables[t], ALU.mult)
            pairs = ks_bf[:].bitcast(F32)
            turned = ps.tile([P, 2, P], F32, name="turned%d" % t, tag="bank%d" % (5 + t % 2))
            for u in range(2):
                nc.tensor.transpose(turned[:, u, :], pairs[:, u : I // 2 : 2], ident[:])
            return turned

        def weave_turned(turned, pairs):
            nc.scalar.copy(pairs.rearrange("s (p u) -> s p u", u=2), turned[:].rearrange("s u p -> s p u"))
            return pairs.bitcast(BF16)

        def quantize_ks(t, ks_in, scales_tag):
            ks_scales.append(sb.tile([P, P], U8, name="ks_scales%d" % t, tag=scales_tag, align_bytes=ALIGN))
            nc.vector.quantize_mx(out=ks_codes[t][:].bitcast(FP8X4), scales=ks_scales[t][:], in_=ks_in)

        for t in range(2):
            gather(t)
            turned = scale_and_turn(t)
            ks_pairs = sb.tile([P, I // 2], F32, name="ks_pairs%d" % t, align_bytes=ALIGN)
            quantize_ks(t, weave_turned(turned, ks_pairs[:]), "ks_scales%d" % t)
        weave_key_planes(nc.scalar.copy, 0)
        gather(2)
        turned2 = scale_and_turn(2)
        gather(LAST)
        last_turned = ps.tile([P, PACK, P], F32, name="last_turned", tag="bank7")
        for r in range(PACK):
            nc.tensor.transpose(last_turned[:, r, :], picked[1][:, 1, r:I:PACK], ident[:])
        weave_key_planes(nc.vector.tensor_copy, 1)

        def quantize_keys(u, scales_tag):
            key_scales.append(sb.tile([P, 2 * P], U8, name="key_scales%d" % u, tag=scales_tag, align_bytes=ALIGN))
            nc.vector.quantize_mx(
                out=key_codes[u][:].bitcast(FP8X4),
                scales=key_scales[u][:],
                in_=key_bf[:, 2 * u : 2 * u + 2, :, :].rearrange("p r s t -> p (r s t)"),
            )

        cent_codes = sb.tile([P, M], U32, name="cent_codes", align_bytes=ALIGN)
        cent_scales = sb.tile([P, M], U8, name="cent_scales", align_bytes=ALIGN)
        cent_bf = sb.tile([P, M * PACK], BF16, name="cent_bf", tag="ks_bf1", align_bytes=ALIGN)
        for c in range(PIECES):
            weave(nc.scalar.copy, cent_bf[:, c * PIECE * PACK : (c + 1) * PIECE * PACK], cent_raw[c][:])

        def quantize_cent(m0, m1):
            nc.vector.quantize_mx(
                out=cent_codes[:, m0:m1].bitcast(FP8X4),
                scales=cent_scales[:, m0:m1],
                in_=cent_bf[:, m0 * PACK : m1 * PACK],
            )

        cent_spans = ((0, 2 * PIECE), (2 * PIECE, 3 * PIECE), (3 * PIECE, M))
        quantize_cent(*cent_spans[0])
        quantize_keys(0, "key_scales0")
        quantize_cent(*cent_spans[1])
        quantize_cent(*cent_spans[2])
        quantize_keys(1, "ks_bf1")

        late = sb.tile([P, I + I // 2], F32, name="late", tag="cent_raw%d" % (PIECES - 1), align_bytes=ALIGN)
        last_keys = late[:, 0:I]
        nc.scalar.copy(last_keys.rearrange("s (p r) -> s p r", r=PACK), last_turned[:].rearrange("s r p -> s p r"))
        last_ks = sb.tile([P, I], BF16, name="last_ks", tag="key_bf", align_bytes=ALIGN)
        nc.gpsimd.tensor_tensor(last_ks[:], last_keys, last_table[:].rearrange("s p r -> s (p r)"), ALU.mult)
        ks_in2 = weave_turned(turned2, late[:, I : I + I // 2])

        neg_max = sb.tile([P, PACK], F32, name="neg_max")
        sums = sb.tile([P, PACK], F32, name="sums")
        inv_sums = sb.tile([P, PACK], F32, name="inv_sums")
        exps = [sb.tile([P, M], F32, name="exps%d" % r, tag="exps%d" % r, align_bytes=ALIGN) for r in range(PACK)]
        scores = [ps.tile([P, M], F32, name="scores%d" % r, tag="bank%d" % r) for r in range(PACK)]
        w_rows = sb.tile([P, PACK, M], BF16, name="w_rows")

        def score_product(acc, r, m0, m1):
            cols = slice(r % 2 * P, (r % 2 + 1) * P)
            mx_product(
                nc,
                acc[:, m0:m1],
                key_codes[r // 2][:, cols],
                key_scales[r // 2][:, cols],
                cent_codes[:, m0:m1],
                cent_scales[:, m0:m1],
            )

        def softmax_terms(r):
            for m0, m1 in cent_spans if r == 0 else ((0, M),):
                score_product(scores[r], r, m0, m1)
            nc.vector.tensor_reduce(neg_max[:, r : r + 1], scores[r][:], AXIS.X, ALU.max, negate=True)
            nc.scalar.activation(
                exps[r][:], scores[r][:], ACT.Exp, bias=neg_max[:, r : r + 1], accum_out=sums[:, r : r + 1]
            )

        def invert(r0, r1):
            nc.vector.reciprocal(inv_sums[:, r0:r1], sums[:, r0:r1])

        def weigh(engine, r, m0, m1):
            engine.tensor_scalar(
                w_rows[:, r, m0:m1],
                exps[r][:, m0:m1],
                inv_sums[:, r : r + 1],
                fac4[:, r : r + 1],
                ALU.mult,
                ALU.mult,
            )

        for r in range(LAST):
            softmax_terms(r)
        invert(0, 1)
        softmax_terms(LAST)
        invert(1, LAST)

        warm_up = ps.tile([P, M], F32, name="warm_up", tag="bank%d" % LAST)
        for r in range(2):
            score_product(warm_up, r, 0, M)

        weigh(nc.gpsimd, 0, 0, M)
        factor1 = sb.tile([P, 1], F32, name="factor1")
        nc.vector.tensor_tensor(factor1[:], inv_sums[:, 1:2], fac4[:, 1:2], ALU.mult)
        nc.scalar.activation(w_rows[:, 1, :], exps[1][:], ACT.Copy, scale=factor1[:])
        weigh(nc.vector, 2, 0, M)
        quantize_ks(2, ks_in2, "ks_scales2")
        invert(LAST, PACK)
        quantize_ks(LAST, last_ks[:], "exps2")
        for h in range(2):
            weigh(nc.vector, LAST, h * HALF, (h + 1) * HALF)

        w_in = [sb.tile([P, HALF * PACK], BF16, name="w_in%d" % h, align_bytes=ALIGN) for h in range(2)]
        w_codes = [sb.tile([P, HALF], U32, name="w_codes%d" % h, align_bytes=ALIGN) for h in range(2)]
        w_scales = [sb.tile([P, HALF], U8, name="w_scales%d" % h, align_bytes=ALIGN) for h in range(2)]
        weave(nc.vector.tensor_copy, w_in[0][:], w_rows[:, :, 0:HALF])
        weave(nc.scalar.copy, w_in[1][:], w_rows[:, :, HALF:M])
        for h in range(2):
            nc.vector.quantize_mx(out=w_codes[h][:].bitcast(FP8X4), scales=w_scales[h][:], in_=w_in[h][:])

        out_rows = out.rearrange("(p t) m -> p t m", t=PACK)
        copies = (nc.scalar.copy, nc.vector.tensor_copy)
        for h in range(2):
            cols = slice(h * HALF, (h + 1) * HALF)
            for t0 in range(0, PACK, 2):
                first_pair = h == 0 and t0 == 0
                res = sb.tile([P, 2, HALF], F32, name="res%d%d" % (h, t0))
                for e in range(2):
                    t = t0 + e
                    acc = ps.tile([P, HALF], F32, name="acc%d%d" % (h, t), tag="bank%d" % (7 - PACK * h - t))
                    mx_product(nc, acc[:], ks_codes[t][:], ks_scales[t][:], w_codes[h][:], w_scales[h][:])
                    copies[e](res[:, e, :], acc[:])
                    if first_pair:
                        nc.sync.dma_start(out=out_rows[:, t, cols], in_=res[:, e, :])
                if not first_pair:
                    nc.sync.dma_start(out=out_rows[:, t0 : t0 + 2, cols], in_=res[:])
